import numpy as np
import ml_dtypes


def mxq(x, axis, fmt="e4m3"):
    dtype, down = {"e4m3": (ml_dtypes.float8_e4m3fn, 7), "e5m2": (ml_dtypes.float8_e5m2, 14)}[fmt]
    v = np.moveaxis(np.asarray(x, np.float32).astype(ml_dtypes.bfloat16).astype(np.float64), axis, -1)
    blocks = v.reshape(v.shape[:-1] + (-1, 32))
    amax = np.abs(blocks).max(-1, keepdims=True)
    byte = np.maximum(np.where(amax > 0, np.frexp(amax)[1] - 1 + 127, 0) - down, 1)
    scale = np.exp2(byte - 127.0)
    codes = (blocks / scale).astype(np.float32).astype(dtype).astype(np.float64)
    return np.moveaxis((codes * scale).reshape(v.shape), -1, axis)


WIDE = False


def mx_kscale(k):
    if not WIDE:
        return np.ones(k)
    levels = np.array([10, -10, 5, -5, 0])
    if k % 512:
        return np.exp2(np.random.permutation(np.resize(levels, k // 32))).repeat(32)
    a = np.empty((k // 512, 16))
    for p in range(k // 512):
        a[p, :8] = np.random.permutation(np.resize(levels, 8))
        for g in range(8):
            far = levels[np.abs(levels - a[p, g]) >= 10]
            a[p, g + 8] = far[np.random.randint(len(far))]
    return np.exp2(a.ravel()).repeat(32)


def f64(x):
    return np.asarray(x).astype(np.float64)


def striped(idx):
    return np.tile(idx.reshape(-1, 16).T, (8, 1)).astype(np.uint16)


def unstriped(offs):
    return offs[:16].T.reshape(-1).astype(np.int64)


def pack_weight(w):
    k, n = w.shape
    w = f64(np.asarray(w, np.float32).astype(ml_dtypes.bfloat16)).reshape(k // 32, 32, n)
    amax = np.abs(w).max(1)
    byte = np.clip(np.where(amax > 0, np.frexp(amax)[1] - 1 + 127 - 7, 1), 1, 254)
    scaled = (w * np.exp2(127.0 - byte)[:, None, :]).reshape(k, n).astype(np.float32)
    words = np.ascontiguousarray(scaled.reshape(k // 512, 128, 4, n).transpose(0, 1, 3, 2)).astype(ml_dtypes.float8_e4m3fn).view(np.uint8)
    return words, np.ascontiguousarray(byte.astype(np.uint8).reshape(k // 512, 16, n))


def unpack_weight(words, scales):
    g, p, n, _ = words.shape
    vals = np.ascontiguousarray(words).view(ml_dtypes.float8_e4m3fn).astype(np.float64) * np.repeat(np.exp2(scales.astype(np.float64) - 127.0), 8, axis=1)[..., None]
    return vals.transpose(0, 1, 3, 2).reshape(g * 512, n)


def sigmoid(v):
    return 1.0 / (1.0 + np.exp(-np.maximum(v, -700.0)))


K, T, S, N = 1024, 1024, 512, 128


def setup_inputs():
    n = np.random.standard_normal
    s = mx_kscale(K)[:, None]
    packed_xT = pack_weight(n((K, T)) * s)
    return {
        "x_words": packed_xT[0],
        "x_scales": packed_xT[1],
        "res": n((N, T)).astype(np.float32),
        "w1": (n((K, N)) / np.sqrt(K) / s).astype(np.float32),
        "w2": (n((K, N)) / np.sqrt(K) / s).astype(np.float32),
        "offs": striped(np.random.permutation(T)[:S]),
    }


def reference(x_words, x_scales, res, w1, w2, offs):
    r = f64(res)[:, unstriped(offs)]
    xq = unpack_weight(x_words, x_scales)[:, unstriped(offs)]
    g = sigmoid(mxq(f64(w2), 0, "e4m3").T @ xq)
    y = np.tanh(mxq(f64(w1), 0, "e4m3").T @ xq)
    return r + g * (y - r)

@@ -1,0 +1,147 @@
+from contextlib import ExitStack
+
+import concourse.mybir as mybir
+
+K, T, S, N = 1024, 1024, 512, 128
+FLOPS = 2 * 2 * K * N * S
+
+F32 = mybir.dt.float32
+BF16 = mybir.dt.bfloat16
+I32 = mybir.dt.int32
+U32 = mybir.dt.uint32
+U16 = mybir.dt.uint16
+U8 = mybir.dt.uint8
+FP8X4 = mybir.dt.float8_e4m3fn_x4
+ACT = mybir.ActivationFunctionType
+ALU = mybir.AluOpType
+
+P = 128
+PACK = 4
+K_PASS = P * PACK
+PASSES = K // K_PASS
+HALVES = 2
+H = S // HALVES
+
+
+def tile_picked_highway_tanh_p_kernel(tc, x_words, x_scales, res, w1, w2, offs, out):
+    nc = tc.nc
+    with ExitStack() as ctx:
+        keep = ctx.enter_context(tc.tile_pool(name="keep", bufs=1))
+        psum = ctx.enter_context(tc.psum_pool(name="psum", bufs=1))
+
+        offsets = keep.tile([P, S // 16], U16, name="offsets")
+        nc.sync.dma_start(offsets[:], offs)
+
+        def part(h):
+            return offsets[:, h * H // 16 : (h + 1) * H // 16]
+
+        scale_table = keep.tile([P, T], U8, name="scale_table", align_bytes=64)
+        nc.vector.memset(scale_table[:].bitcast(I32), 0)
+        for q in range(4):
+            nc.scalar.dma_start(
+                scale_table[32 * q : 32 * q + 4 * PASSES, :].bitcast(I32),
+                x_scales[:, 4 * q : 4 * q + 4, :].bitcast(I32),
+            )
+
+        word_table = [keep.tile([P, T], I32, name=f"word_table{z}", align_bytes=64) for z in range(PASSES)]
+        raw = {}
+        for name in ("w1", "w2"):
+            for z in range(PASSES):
+                raw[name, z] = keep.tile([P, PACK, N], F32, name=f"raw_{name}_{z}")
+        res_table = keep.tile([P, T], F32, name="res_table", align_bytes=64)
+
+        def load_words(z):
+            nc.sync.dma_start(word_table[z][:], x_words[z].rearrange("p n t -> p (n t)").bitcast(I32))
+
+        def load_weight(name, w, z):
+            rows = w[z * K_PASS : (z + 1) * K_PASS, :]
+            nc.sync.dma_start(raw[name, z][:], rows.rearrange("(p j) m -> p j m", j=PACK))
+
+        load_words(0)
+        load_weight("w1", w1, 0)
+        load_weight("w1", w1, 1)
+        load_words(1)
+        load_weight("w2", w2, 0)
+        load_weight("w2", w2, 1)
+        nc.sync.dma_start(res_table[:], res)
+
+        x_scale = keep.tile([P, S], U8, name="x_scale", align_bytes=64)
+        x_codes = [keep.tile([P, S], U32, name=f"x_codes{z}", align_bytes=64) for z in range(PASSES)]
+        grouped = {}
+        w_codes = {}
+        w_scale = {}
+        for name in ("w1", "w2"):
+            for z in range(PASSES):
+                grouped[name, z] = keep.tile([P, N, PACK], BF16, name=f"grouped_{name}_{z}", align_bytes=64)
+                w_codes[name, z] = keep.tile([P, N], U32, name=f"codes_{name}_{z}", align_bytes=64)
+                w_scale[name, z] = keep.tile([P, N], U8, name=f"scale_{name}_{z}", align_bytes=64)
+
+        def cast(name, z):
+            nc.scalar.activation(
+                grouped[name, z][:].rearrange("p (c i) j -> p c j i", i=4),
+                raw[name, z][:].rearrange("p j (c i) -> p c j i", i=4),
+                ACT.Copy,
+            )
+
+        def quantize(name, z):
+            nc.vector.quantize_mx(
+                out=w_codes[name, z][:].bitcast(FP8X4),
+                scales=w_scale[name, z][:],
+                in_=grouped[name, z][:].rearrange("p m j -> p (m j)"),
+            )
+
+        def gather_words(z, h):
+            nc.vector.tensor_copy(x_codes[z][:, h * H : (h + 1) * H], word_table[z][:].bitcast(U32).indirect(part(h)))
+
+        acc = {}
+        for name in ("w1", "w2"):
+            for h in range(HALVES):
+                acc[name, h] = psum.tile([P, H], F32, name=f"acc_{name}_{h}")
+
+        def product(name, z, h):
+            cols = slice(h * H, (h + 1) * H)
+            nc.tensor.matmul_mx(
+                out=acc[name, h][:],
+                lhsT=w_codes[name, z][:].bitcast(FP8X4),
+                lhsT_scale=w_scale[name, z][:],
+                rhs=x_codes[z][:, cols].bitcast(FP8X4),
+                rhs_scale=x_scale[4 * z : P, cols],
+                start=(z == 0),
+                stop=(z == PASSES - 1),
+            )
+
+        nc.vector.tensor_copy(x_scale[:], scale_table[:].indirect(offsets[:]))
+        nc.vector.tensor_copy(x_codes[0][:], word_table[0][:].bitcast(U32).indirect(offsets[:]))
+        cast("w1", 0)
+        cast("w1", 1)
+        quantize("w1", 0)
+        gather_words(1, 0)
+        quantize("w1", 1)
+        gather_words(1, 1)
+        cast("w2", 0)
+        cast("w2", 1)
+        y = [keep.tile([P, H], F32, name=f"y{h}") for h in range(HALVES)]
+        t = [keep.tile([P, H], F32, name=f"t{h}") for h in range(HALVES)]
+        for h in range(HALVES):
+            product("w1", 0, h)
+        for h in range(HALVES):
+            product("w1", 1, h)
+            nc.scalar.activation(y[h][:], acc["w1", h][:], ACT.Tanh)
+        quantize("w2", 0)
+        quantize("w2", 1)
+        for h in range(HALVES):
+            product("w2", 0, h)
+        for h in range(HALVES):
+            product("w2", 1, h)
+            nc.scalar.activation(t[h][:], acc["w2", h][:], ACT.Tanh, scale=0.5)
+
+        d = [keep.tile([P, H], F32, name=f"d{h}") for h in range(HALVES)]
+        e = [keep.tile([P, H], F32, name=f"e{h}") for h in range(HALVES)]
+        o = [keep.tile([P, H], F32, name=f"o{h}") for h in range(HALVES)]
+        for h in range(HALVES):
+            nc.vector.tensor_tensor(d[h][:], res_table[:].indirect(part(h)), y[h][:], ALU.subtract)
+        for h in range(HALVES):
+            nc.vector.scalar_tensor_tensor(e[h][:], t[h][:], -1.0, d[h][:], ALU.add, ALU.mult)
+        for h in range(HALVES):
+            nc.vector.scalar_tensor_tensor(o[h][:], e[h][:], -0.5, y[h][:], ALU.mult, ALU.add)
+            nc.sync.dma_start(out[:, h * H : (h + 1) * H], o[h][:])

@@ -29,26 +29,25 @@ def tile_picked_highway_tanh_p_kernel(tc, x_words, x_scales, res, w1, w2, offs, 
         keep = ctx.enter_context(tc.tile_pool(name="keep", bufs=1))
         psum = ctx.enter_context(tc.psum_pool(name="psum", bufs=1))
 
+        def tile(shape, dtype, name, tag=None):
+            return keep.tile(shape, dtype, name=name, tag=tag or name, align_bytes=64)
+
         offsets = keep.tile([P, S // 16], U16, name="offsets")
         nc.sync.dma_start(offsets[:], offs)
 
         def part(h):
             return offsets[:, h * H // 16 : (h + 1) * H // 16]
 
-        scale_table = keep.tile([P, T], U8, name="scale_table", align_bytes=64)
+        scale_table = tile([P, T], U8, "scale_table")
         nc.vector.memset(scale_table[:].bitcast(I32), 0)
-        for q in range(4):
-            nc.scalar.dma_start(
-                scale_table[32 * q : 32 * q + 4 * PASSES, :].bitcast(I32),
-                x_scales[:, 4 * q : 4 * q + 4, :].bitcast(I32),
-            )
+        warm_in = tile([P, 1], F32, "warm_in")
+        warm_out = tile([P, 1], F32, "warm_out")
+        nc.vector.memset(warm_in[:], 0.0)
+        nc.scalar.activation(warm_out[:], warm_in[:], ACT.Tanh)
 
-        word_table = [keep.tile([P, T], I32, name=f"word_table{z}", align_bytes=64) for z in range(PASSES)]
-        raw = {}
-        for name in ("w1", "w2"):
-            for z in range(PASSES):
-                raw[name, z] = keep.tile([P, PACK, N], F32, name=f"raw_{name}_{z}")
-        res_table = keep.tile([P, T], F32, name="res_table", align_bytes=64)
+        word_table = [tile([P, T], I32, f"word_table{z}") for z in range(PASSES)]
+        raw = {(name, z): tile([P, PACK, N], F32, f"raw_{name}_{z}") for name in ("w1", "w2") for z in range(PASSES)}
+        res_table = tile([P, T], F32, "res_table")
 
         def load_words(z):
             nc.sync.dma_start(word_table[z][:], x_words[z].rearrange("p n t -> p (n t)").bitcast(I32))
@@ -57,7 +56,15 @@ def tile_picked_highway_tanh_p_kernel(tc, x_words, x_scales, res, w1, w2, offs, 
             rows = w[z * K_PASS : (z + 1) * K_PASS, :]
             nc.sync.dma_start(raw[name, z][:], rows.rearrange("(p j) m -> p j m", j=PACK))
 
+        def load_scales(q, eng):
+            eng.dma_start(
+                scale_table[32 * q : 32 * q + 4 * PASSES, :].bitcast(I32),
+                x_scales[:, 4 * q : 4 * q + 4, :].bitcast(I32),
+            )
+
         load_words(0)
+        for q in range(4):
+            load_scales(q, nc.sync)
         load_weight("w1", w1, 0)
         load_weight("w1", w1, 1)
         load_words(1)
@@ -65,16 +72,16 @@ def tile_picked_highway_tanh_p_kernel(tc, x_words, x_scales, res, w1, w2, offs, 
         load_weight("w2", w2, 1)
         nc.sync.dma_start(res_table[:], res)
 
-        x_scale = keep.tile([P, S], U8, name="x_scale", align_bytes=64)
-        x_codes = [keep.tile([P, S], U32, name=f"x_codes{z}", align_bytes=64) for z in range(PASSES)]
+        x_scale = tile([P, S], U8, "x_scale")
+        x_codes = {}
         grouped = {}
         w_codes = {}
         w_scale = {}
         for name in ("w1", "w2"):
             for z in range(PASSES):
-                grouped[name, z] = keep.tile([P, N, PACK], BF16, name=f"grouped_{name}_{z}", align_bytes=64)
-                w_codes[name, z] = keep.tile([P, N], U32, name=f"codes_{name}_{z}", align_bytes=64)
-                w_scale[name, z] = keep.tile([P, N], U8, name=f"scale_{name}_{z}", align_bytes=64)
+                grouped[name, z] = tile([P, N, PACK], BF16, f"grouped_{name}_{z}")
+                w_codes[name, z] = tile([P, N], U32, f"codes_{name}_{z}")
+                w_scale[name, z] = tile([P, N], U8, f"scale_{name}_{z}")
 
         def cast(name, z):
             nc.scalar.activation(
@@ -90,58 +97,58 @@ def tile_picked_highway_tanh_p_kernel(tc, x_words, x_scales, res, w1, w2, offs, 
                 in_=grouped[name, z][:].rearrange("p m j -> p (m j)"),
             )
 
-        def gather_words(z, h):
-            nc.vector.tensor_copy(x_codes[z][:, h * H : (h + 1) * H], word_table[z][:].bitcast(U32).indirect(part(h)))
-
         acc = {}
         for name in ("w1", "w2"):
             for h in range(HALVES):
                 acc[name, h] = psum.tile([P, H], F32, name=f"acc_{name}_{h}")
 
         def product(name, z, h):
-            cols = slice(h * H, (h + 1) * H)
             nc.tensor.matmul_mx(
                 out=acc[name, h][:],
                 lhsT=w_codes[name, z][:].bitcast(FP8X4),
                 lhsT_scale=w_scale[name, z][:],
-                rhs=x_codes[z][:, cols].bitcast(FP8X4),
-                rhs_scale=x_scale[4 * z : P, cols],
+                rhs=x_codes[z, h].bitcast(FP8X4),
+                rhs_scale=x_scale[4 * z : P, h * H : (h + 1) * H],
                 start=(z == 0),
                 stop=(z == PASSES - 1),
             )
 
+        x_first = tile([P, S], U32, "x_first")
+        nc.vector.tensor_copy(x_first[:], word_table[0][:].bitcast(U32).indirect(offsets[:]))
         nc.vector.tensor_copy(x_scale[:], scale_table[:].indirect(offsets[:]))
-        nc.vector.tensor_copy(x_codes[0][:], word_table[0][:].bitcast(U32).indirect(offsets[:]))
-        cast("w1", 0)
-        cast("w1", 1)
-        quantize("w1", 0)
-        gather_words(1, 0)
-        quantize("w1", 1)
-        gather_words(1, 1)
-        cast("w2", 0)
-        cast("w2", 1)
-        y = [keep.tile([P, H], F32, name=f"y{h}") for h in range(HALVES)]
-        t = [keep.tile([P, H], F32, name=f"t{h}") for h in range(HALVES)]
+        for h in range(HALVES):
+            x_codes[0, h] = x_first[:, h * H : (h + 1) * H]
+        for z in range(PASSES):
+            cast("w1", z)
+            quantize("w1", z)
+        for h in range(HALVES):
+            second = tile([P, H], U32, f"x_second{h}", tag=f"grouped_w1_{h}")
+            nc.vector.tensor_copy(second[:], word_table[1][:].bitcast(U32).indirect(part(h)))
+            x_codes[1, h] = second[:]
+        for z in range(PASSES):
+            cast("w2", z)
+            quantize("w2", z)
+        y_all = tile([P, S], F32, "y_all", tag="raw_w2_1")
+        y = [y_all[:, h * H : (h + 1) * H] for h in range(HALVES)]
+        t = [tile([P, H], F32, f"t{h}") for h in range(HALVES)]
         for h in range(HALVES):
             product("w1", 0, h)
         for h in range(HALVES):
             product("w1", 1, h)
-            nc.scalar.activation(y[h][:], acc["w1", h][:], ACT.Tanh)
-        quantize("w2", 0)
-        quantize("w2", 1)
+            nc.scalar.activation(y[h], acc["w1", h][:], ACT.Tanh)
         for h in range(HALVES):
             product("w2", 0, h)
         for h in range(HALVES):
             product("w2", 1, h)
             nc.scalar.activation(t[h][:], acc["w2", h][:], ACT.Tanh, scale=0.5)
 
-        d = [keep.tile([P, H], F32, name=f"d{h}") for h in range(HALVES)]
-        e = [keep.tile([P, H], F32, name=f"e{h}") for h in range(HALVES)]
-        o = [keep.tile([P, H], F32, name=f"o{h}") for h in range(HALVES)]
+        d = [tile([P, H], F32, f"d{h}", tag=f"grouped_w2_{1 - h}") for h in range(HALVES)]
+        e = [tile([P, H], F32, f"e{h}") for h in range(HALVES)]
+        o = [tile([P, H], F32, f"o{h}") for h in range(HALVES)]
         for h in range(HALVES):
-            nc.vector.tensor_tensor(d[h][:], res_table[:].indirect(part(h)), y[h][:], ALU.subtract)
+            nc.vector.tensor_tensor(d[h][:], res_table[:].indirect(part(h)), y[h], ALU.subtract)
         for h in range(HALVES):
             nc.vector.scalar_tensor_tensor(e[h][:], t[h][:], -1.0, d[h][:], ALU.add, ALU.mult)
         for h in range(HALVES):
-            nc.vector.scalar_tensor_tensor(o[h][:], e[h][:], -0.5, y[h][:], ALU.mult, ALU.add)
+            nc.vector.scalar_tensor_tensor(o[h][:], e[h][:], -0.5, y[h], ALU.mult, ALU.add)
             nc.sync.dma_start(out[:, h * H : (h + 1) * H], o[h][:])

@@ -33,44 +33,27 @@ def tile_picked_highway_tanh_p_kernel(tc, x_words, x_scales, res, w1, w2, offs, 
             return keep.tile(shape, dtype, name=name, tag=tag or name, align_bytes=64)
 
         offsets = keep.tile([P, S // 16], U16, name="offsets")
-        nc.sync.dma_start(offsets[:], offs)
 
-        def part(h):
-            return offsets[:, h * H // 16 : (h + 1) * H // 16]
+        def part(a, b):
+            return offsets[:, a // 16 : b // 16]
 
         scale_table = tile([P, T], U8, "scale_table")
-        nc.vector.memset(scale_table[:].bitcast(I32), 0)
-        warm_in = tile([P, 1], F32, "warm_in")
-        warm_out = tile([P, 1], F32, "warm_out")
-        nc.vector.memset(warm_in[:], 0.0)
-        nc.scalar.activation(warm_out[:], warm_in[:], ACT.Tanh)
-
         word_table = [tile([P, T], I32, f"word_table{z}") for z in range(PASSES)]
         raw = {(name, z): tile([P, PACK, N], F32, f"raw_{name}_{z}") for name in ("w1", "w2") for z in range(PASSES)}
         res_table = tile([P, T], F32, "res_table")
 
-        def load_words(z):
-            nc.sync.dma_start(word_table[z][:], x_words[z].rearrange("p n t -> p (n t)").bitcast(I32))
+        def load_words(z, eng=nc.sync):
+            eng.dma_start(word_table[z][:], x_words[z].rearrange("p n t -> p (n t)").bitcast(I32))
 
-        def load_weight(name, w, z):
+        def load_weight(name, w, z, eng=nc.sync):
             rows = w[z * K_PASS : (z + 1) * K_PASS, :]
-            nc.sync.dma_start(raw[name, z][:], rows.rearrange("(p j) m -> p j m", j=PACK))
+            eng.dma_start(raw[name, z][:], rows.rearrange("(p j) m -> p j m", j=PACK))
 
         def load_scales(q, eng):
             eng.dma_start(
                 scale_table[32 * q : 32 * q + 4 * PASSES, :].bitcast(I32),
                 x_scales[:, 4 * q : 4 * q + 4, :].bitcast(I32),
             )
-
-        load_words(0)
-        for q in range(4):
-            load_scales(q, nc.sync)
-        load_weight("w1", w1, 0)
-        load_weight("w1", w1, 1)
-        load_words(1)
-        load_weight("w2", w2, 0)
-        load_weight("w2", w2, 1)
-        nc.sync.dma_start(res_table[:], res)
 
         x_scale = tile([P, S], U8, "x_scale")
         x_codes = {}
@@ -83,12 +66,19 @@ def tile_picked_highway_tanh_p_kernel(tc, x_words, x_scales, res, w1, w2, offs, 
                 w_codes[name, z] = tile([P, N], U32, f"codes_{name}_{z}")
                 w_scale[name, z] = tile([P, N], U8, f"scale_{name}_{z}")
 
-        def cast(name, z):
-            nc.scalar.activation(
+        def cast_views(name, z):
+            return (
                 grouped[name, z][:].rearrange("p (c i) j -> p c j i", i=4),
                 raw[name, z][:].rearrange("p j (c i) -> p c j i", i=4),
-                ACT.Copy,
             )
+
+        def cast(name, z):
+            dst, src = cast_views(name, z)
+            nc.scalar.activation(dst, src, ACT.Copy)
+
+        def cast_vector(name, z):
+            dst, src = cast_views(name, z)
+            nc.vector.tensor_copy(dst, src)
 
         def quantize(name, z):
             nc.vector.quantize_mx(
@@ -97,58 +87,74 @@ def tile_picked_highway_tanh_p_kernel(tc, x_words, x_scales, res, w1, w2, offs, 
                 in_=grouped[name, z][:].rearrange("p m j -> p (m j)"),
             )
 
-        acc = {}
-        for name in ("w1", "w2"):
-            for h in range(HALVES):
-                acc[name, h] = psum.tile([P, H], F32, name=f"acc_{name}_{h}")
-
-        def product(name, z, h):
+        def product(bank, name, z, a, b):
             nc.tensor.matmul_mx(
-                out=acc[name, h][:],
+                out=bank[:],
                 lhsT=w_codes[name, z][:].bitcast(FP8X4),
                 lhsT_scale=w_scale[name, z][:],
-                rhs=x_codes[z, h].bitcast(FP8X4),
-                rhs_scale=x_scale[4 * z : P, h * H : (h + 1) * H],
+                rhs=x_codes[z][:, a:b].bitcast(FP8X4),
+                rhs_scale=x_scale[4 * z : P, a:b],
                 start=(z == 0),
                 stop=(z == PASSES - 1),
             )
 
-        x_first = tile([P, S], U32, "x_first")
-        nc.vector.tensor_copy(x_first[:], word_table[0][:].bitcast(U32).indirect(offsets[:]))
+        g_cuts = ((0, 256), (256, 512))
+        y_cuts = ((0, 256), (256, 512))
+        t_cuts = ((0, 256), (256, 512))
+        d_cuts = ((0, 256), (256, 512))
+        nc.vector.memset(scale_table[:].bitcast(I32), 0)
+        nc.sync.dma_start(offsets[:], offs)
+        load_words(0)
+        for q in range(4):
+            load_scales(q, nc.sync)
+        load_weight("w1", w1, 0)
+        load_weight("w1", w1, 1)
+        load_words(1)
+        load_weight("w2", w2, 0)
+        load_weight("w2", w2, 1)
+        nc.sync.dma_start(res_table[:], res)
+
+        x_codes[0] = tile([P, S], U32, "x_first")
+        nc.vector.tensor_copy(x_codes[0][:], word_table[0][:].bitcast(U32).indirect(offsets[:]))
         nc.vector.tensor_copy(x_scale[:], scale_table[:].indirect(offsets[:]))
-        for h in range(HALVES):
-            x_codes[0, h] = x_first[:, h * H : (h + 1) * H]
         for z in range(PASSES):
             cast("w1", z)
             quantize("w1", z)
-        for h in range(HALVES):
-            second = tile([P, H], U32, f"x_second{h}", tag=f"grouped_w1_{h}")
-            nc.vector.tensor_copy(second[:], word_table[1][:].bitcast(U32).indirect(part(h)))
-            x_codes[1, h] = second[:]
+        x_codes[1] = tile([P, S], U32, "x_second", tag="grouped_w1_1")
+        for a, b in g_cuts:
+            nc.vector.tensor_copy(x_codes[1][:, a:b], word_table[1][:].bitcast(U32).indirect(part(a, b)))
         for z in range(PASSES):
             cast("w2", z)
             quantize("w2", z)
-        y_all = tile([P, S], F32, "y_all", tag="raw_w2_1")
-        y = [y_all[:, h * H : (h + 1) * H] for h in range(HALVES)]
-        t = [tile([P, H], F32, f"t{h}") for h in range(HALVES)]
-        for h in range(HALVES):
-            product("w1", 0, h)
-        for h in range(HALVES):
-            product("w1", 1, h)
-            nc.scalar.activation(y[h], acc["w1", h][:], ACT.Tanh)
-        for h in range(HALVES):
-            product("w2", 0, h)
-        for h in range(HALVES):
-            product("w2", 1, h)
-            nc.scalar.activation(t[h][:], acc["w2", h][:], ACT.Tanh, scale=0.5)
+        y = tile([P, S], F32, "y", tag="raw_w2_0")
+        t = tile([P, S], F32, "t")
+        y_bank = {cut: psum.tile([P, cut[1] - cut[0]], F32, name=f"y_bank{cut[0]}") for cut in y_cuts}
+        t_bank = {cut: psum.tile([P, cut[1] - cut[0]], F32, name=f"t_bank{cut[0]}") for cut in t_cuts}
+        for a, b in y_cuts:
+            product(y_bank[a, b], "w1", 0, a, b)
+        for a, b in y_cuts:
+            product(y_bank[a, b], "w1", 1, a, b)
+            nc.scalar.activation(y[:, a:b], y_bank[a, b][:], ACT.Tanh)
+        for a, b in t_cuts:
+            product(t_bank[a, b], "w2", 0, a, b)
+        for a, b in t_cuts:
+            product(t_bank[a, b], "w2", 1, a, b)
+            nc.scalar.activation(t[:, a:b], t_bank[a, b][:], ACT.Tanh, scale=0.5)
 
-        d = [tile([P, H], F32, f"d{h}", tag=f"grouped_w2_{1 - h}") for h in range(HALVES)]
-        e = [tile([P, H], F32, f"e{h}") for h in range(HALVES)]
-        o = [tile([P, H], F32, f"o{h}") for h in range(HALVES)]
-        for h in range(HALVES):
-            nc.vector.tensor_tensor(d[h][:], res_table[:].indirect(part(h)), y[h], ALU.subtract)
-        for h in range(HALVES):
-            nc.vector.scalar_tensor_tensor(e[h][:], t[h][:], -1.0, d[h][:], ALU.add, ALU.mult)
-        for h in range(HALVES):
-            nc.vector.scalar_tensor_tensor(o[h][:], e[h][:], -0.5, y[h], ALU.mult, ALU.add)
-            nc.sync.dma_start(out[:, h * H : (h + 1) * H], o[h][:])
+        d = tile([P, S], F32, "d")
+        e = tile([P, S], F32, "e")
+        o = tile([P, S], F32, "o")
+        for a, b in d_cuts:
+            nc.vector.tensor_tensor(d[:, a:b], res_table[:].indirect(part(a, b)), y[:, a:b], ALU.subtract)
+
+        def gate(a, b):
+            nc.vector.scalar_tensor_tensor(e[:, a:b], t[:, a:b], -1.0, d[:, a:b], ALU.add, ALU.mult)
+
+        def finish(a, b):
+            nc.vector.scalar_tensor_tensor(o[:, a:b], e[:, a:b], -0.5, y[:, a:b], ALU.mult, ALU.add)
+            nc.sync.dma_start(out[:, a:b], o[:, a:b])
+
+        for cut in t_cuts:
+            gate(*cut)
+        for cut in t_cuts:
+            finish(*cut)

@@ -19,12 +19,16 @@ P = 128
 PACK = 4
 K_PASS = P * PACK
 PASSES = K // K_PASS
-HALVES = 2
-H = S // HALVES
+QUADRANT = 32
+SCALE_ROWS = 4
+LIST_GROUP = 16
+LINE = 4
+HALVES = ((0, S // 2), (S // 2, S))
 
 
 def tile_picked_highway_tanh_p_kernel(tc, x_words, x_scales, res, w1, w2, offs, out):
     nc = tc.nc
+    weights = {"w1": w1, "w2": w2}
     with ExitStack() as ctx:
         keep = ctx.enter_context(tc.tile_pool(name="keep", bufs=1))
         psum = ctx.enter_context(tc.psum_pool(name="psum", bufs=1))
@@ -32,60 +36,52 @@ def tile_picked_highway_tanh_p_kernel(tc, x_words, x_scales, res, w1, w2, offs, 
         def tile(shape, dtype, name, tag=None):
             return keep.tile(shape, dtype, name=name, tag=tag or name, align_bytes=64)
 
-        offsets = keep.tile([P, S // 16], U16, name="offsets")
+        offsets = keep.tile([P, S // LIST_GROUP], U16, name="offsets")
 
-        def part(a, b):
-            return offsets[:, a // 16 : b // 16]
+        def entries(a, b):
+            return offsets[:, a // LIST_GROUP : b // LIST_GROUP]
 
         scale_table = tile([P, T], U8, "scale_table")
         word_table = [tile([P, T], I32, f"word_table{z}") for z in range(PASSES)]
-        raw = {(name, z): tile([P, PACK, N], F32, f"raw_{name}_{z}") for name in ("w1", "w2") for z in range(PASSES)}
+        raw = {(name, z): tile([P, PACK, N], F32, f"raw_{name}_{z}") for name in weights for z in range(PASSES)}
         res_table = tile([P, T], F32, "res_table")
 
-        def load_words(z, eng=nc.sync):
-            eng.dma_start(word_table[z][:], x_words[z].rearrange("p n t -> p (n t)").bitcast(I32))
+        def load_words(z):
+            nc.sync.dma_start(word_table[z][:], x_words[z].rearrange("p n t -> p (n t)").bitcast(I32))
 
-        def load_weight(name, w, z, eng=nc.sync):
-            rows = w[z * K_PASS : (z + 1) * K_PASS, :]
-            eng.dma_start(raw[name, z][:], rows.rearrange("(p j) m -> p j m", j=PACK))
-
-        def load_scales(q, eng):
-            eng.dma_start(
-                scale_table[32 * q : 32 * q + 4 * PASSES, :].bitcast(I32),
-                x_scales[:, 4 * q : 4 * q + 4, :].bitcast(I32),
+        def load_scales(q):
+            nc.sync.dma_start(
+                scale_table[QUADRANT * q : QUADRANT * q + SCALE_ROWS * PASSES, :].bitcast(I32),
+                x_scales[:, SCALE_ROWS * q : SCALE_ROWS * (q + 1), :].bitcast(I32),
             )
 
+        def load_weight(name, z):
+            rows = weights[name][z * K_PASS : (z + 1) * K_PASS, :]
+            nc.sync.dma_start(raw[name, z][:], rows.rearrange("(p j) m -> p j m", j=PACK))
+
         x_scale = tile([P, S], U8, "x_scale")
-        x_codes = {}
         grouped = {}
         w_codes = {}
         w_scale = {}
-        for name in ("w1", "w2"):
+        for name in weights:
             for z in range(PASSES):
                 grouped[name, z] = tile([P, N, PACK], BF16, f"grouped_{name}_{z}")
                 w_codes[name, z] = tile([P, N], U32, f"codes_{name}_{z}")
                 w_scale[name, z] = tile([P, N], U8, f"scale_{name}_{z}")
 
-        def cast_views(name, z):
-            return (
-                grouped[name, z][:].rearrange("p (c i) j -> p c j i", i=4),
-                raw[name, z][:].rearrange("p j (c i) -> p c j i", i=4),
+        def cast_and_quantize(name, z):
+            nc.scalar.activation(
+                grouped[name, z][:].rearrange("p (c i) j -> p c j i", i=LINE),
+                raw[name, z][:].rearrange("p j (c i) -> p c j i", i=LINE),
+                ACT.Copy,
             )
-
-        def cast(name, z):
-            dst, src = cast_views(name, z)
-            nc.scalar.activation(dst, src, ACT.Copy)
-
-        def cast_vector(name, z):
-            dst, src = cast_views(name, z)
-            nc.vector.tensor_copy(dst, src)
-
-        def quantize(name, z):
             nc.vector.quantize_mx(
                 out=w_codes[name, z][:].bitcast(FP8X4),
                 scales=w_scale[name, z][:],
                 in_=grouped[name, z][:].rearrange("p m j -> p (m j)"),
             )
+
+        x_codes = {}
 
         def product(bank, name, z, a, b):
             nc.tensor.matmul_mx(
@@ -93,68 +89,57 @@ def tile_picked_highway_tanh_p_kernel(tc, x_words, x_scales, res, w1, w2, offs, 
                 lhsT=w_codes[name, z][:].bitcast(FP8X4),
                 lhsT_scale=w_scale[name, z][:],
                 rhs=x_codes[z][:, a:b].bitcast(FP8X4),
-                rhs_scale=x_scale[4 * z : P, a:b],
+                rhs_scale=x_scale[SCALE_ROWS * z : P, a:b],
                 start=(z == 0),
                 stop=(z == PASSES - 1),
             )
 
-        g_cuts = ((0, 256), (256, 512))
-        y_cuts = ((0, 256), (256, 512))
-        t_cuts = ((0, 256), (256, 512))
-        d_cuts = ((0, 256), (256, 512))
         nc.vector.memset(scale_table[:].bitcast(I32), 0)
+
         nc.sync.dma_start(offsets[:], offs)
         load_words(0)
-        for q in range(4):
-            load_scales(q, nc.sync)
-        load_weight("w1", w1, 0)
-        load_weight("w1", w1, 1)
+        for q in (0, 2, 1, 3):
+            load_scales(q)
+        load_weight("w1", 0)
+        load_weight("w1", 1)
         load_words(1)
-        load_weight("w2", w2, 0)
-        load_weight("w2", w2, 1)
+        load_weight("w2", 0)
+        load_weight("w2", 1)
         nc.sync.dma_start(res_table[:], res)
 
         x_codes[0] = tile([P, S], U32, "x_first")
         nc.vector.tensor_copy(x_codes[0][:], word_table[0][:].bitcast(U32).indirect(offsets[:]))
         nc.vector.tensor_copy(x_scale[:], scale_table[:].indirect(offsets[:]))
         for z in range(PASSES):
-            cast("w1", z)
-            quantize("w1", z)
-        x_codes[1] = tile([P, S], U32, "x_second", tag="grouped_w1_1")
-        for a, b in g_cuts:
-            nc.vector.tensor_copy(x_codes[1][:, a:b], word_table[1][:].bitcast(U32).indirect(part(a, b)))
+            cast_and_quantize("w1", z)
+        x_codes[1] = tile([P, S], U32, "x_second", tag="raw_w1_1")
+        for a, b in HALVES:
+            nc.vector.tensor_copy(x_codes[1][:, a:b], word_table[1][:].bitcast(U32).indirect(entries(a, b)))
         for z in range(PASSES):
-            cast("w2", z)
-            quantize("w2", z)
+            cast_and_quantize("w2", z)
+
         y = tile([P, S], F32, "y", tag="raw_w2_0")
-        t = tile([P, S], F32, "t")
-        y_bank = {cut: psum.tile([P, cut[1] - cut[0]], F32, name=f"y_bank{cut[0]}") for cut in y_cuts}
-        t_bank = {cut: psum.tile([P, cut[1] - cut[0]], F32, name=f"t_bank{cut[0]}") for cut in t_cuts}
-        for a, b in y_cuts:
-            product(y_bank[a, b], "w1", 0, a, b)
-        for a, b in y_cuts:
-            product(y_bank[a, b], "w1", 1, a, b)
-            nc.scalar.activation(y[:, a:b], y_bank[a, b][:], ACT.Tanh)
-        for a, b in t_cuts:
-            product(t_bank[a, b], "w2", 0, a, b)
-        for a, b in t_cuts:
-            product(t_bank[a, b], "w2", 1, a, b)
-            nc.scalar.activation(t[:, a:b], t_bank[a, b][:], ACT.Tanh, scale=0.5)
+        half_tanh = tile([P, S], F32, "half_tanh")
+        y_bank = {a: psum.tile([P, b - a], F32, name=f"y_bank{a}") for a, b in HALVES}
+        gate_bank = {a: psum.tile([P, b - a], F32, name=f"gate_bank{a}") for a, b in HALVES}
+        for a, b in HALVES:
+            product(y_bank[a], "w1", 0, a, b)
+        for a, b in HALVES:
+            product(y_bank[a], "w1", 1, a, b)
+            nc.scalar.activation(y[:, a:b], y_bank[a][:], ACT.Tanh)
+        for a, b in HALVES:
+            product(gate_bank[a], "w2", 0, a, b)
+        for a, b in HALVES:
+            product(gate_bank[a], "w2", 1, a, b)
+            nc.scalar.activation(half_tanh[:, a:b], gate_bank[a][:], ACT.Tanh, scale=0.5)
 
-        d = tile([P, S], F32, "d")
-        e = tile([P, S], F32, "e")
-        o = tile([P, S], F32, "o")
-        for a, b in d_cuts:
-            nc.vector.tensor_tensor(d[:, a:b], res_table[:].indirect(part(a, b)), y[:, a:b], ALU.subtract)
-
-        def gate(a, b):
-            nc.vector.scalar_tensor_tensor(e[:, a:b], t[:, a:b], -1.0, d[:, a:b], ALU.add, ALU.mult)
-
-        def finish(a, b):
-            nc.vector.scalar_tensor_tensor(o[:, a:b], e[:, a:b], -0.5, y[:, a:b], ALU.mult, ALU.add)
-            nc.sync.dma_start(out[:, a:b], o[:, a:b])
-
-        for cut in t_cuts:
-            gate(*cut)
-        for cut in t_cuts:
-            finish(*cut)
+        diff = tile([P, S], F32, "diff")
+        gated = tile([P, S], F32, "gated")
+        result = tile([P, S], F32, "result")
+        for a, b in HALVES:
+            nc.vector.tensor_tensor(diff[:, a:b], res_table[:].indirect(entries(a, b)), y[:, a:b], ALU.subtract)
+        for a, b in HALVES:
+            nc.vector.scalar_tensor_tensor(gated[:, a:b], half_tanh[:, a:b], -1.0, diff[:, a:b], ALU.add, ALU.mult)
+        for a, b in HALVES:
+            nc.vector.scalar_tensor_tensor(result[:, a:b], gated[:, a:b], -0.5, y[:, a:b], ALU.mult, ALU.add)
+            nc.sync.dma_start(out[:, a:b], result[:, a:b])

@@ -96,8 +96,8 @@ def tile_picked_highway_tanh_p_kernel(tc, x_words, x_scales, res, w1, w2, offs, 
 
         nc.vector.memset(scale_table[:].bitcast(I32), 0)
 
-        nc.sync.dma_start(offsets[:], offs)
         load_words(0)
+        nc.sync.dma_start(offsets[:], offs)
         for q in (0, 2, 1, 3):
             load_scales(q)
         load_weight("w1", 0)

@@ -24,6 +24,8 @@ SCALE_ROWS = 4
 LIST_GROUP = 16
 LINE = 4
 HALVES = ((0, S // 2), (S // 2, S))
+Y_PIECES = ((0, S // 2), (S // 2, 3 * S // 4), (3 * S // 4, S))
+SCALAR_ENTRIES = 192
 
 
 def tile_picked_highway_tanh_p_kernel(tc, x_words, x_scales, res, w1, w2, offs, out):
@@ -113,20 +115,23 @@ def tile_picked_highway_tanh_p_kernel(tc, x_words, x_scales, res, w1, w2, offs, 
         for z in range(PASSES):
             cast_and_quantize("w1", z)
         x_codes[1] = tile([P, S], U32, "x_second", tag="raw_w1_1")
-        for a, b in HALVES:
+        for a, b in Y_PIECES:
             nc.vector.tensor_copy(x_codes[1][:, a:b], word_table[1][:].bitcast(U32).indirect(entries(a, b)))
         for z in range(PASSES):
             cast_and_quantize("w2", z)
 
         y = tile([P, S], F32, "y", tag="raw_w2_0")
         half_tanh = tile([P, S], F32, "half_tanh")
-        y_bank = {a: psum.tile([P, b - a], F32, name=f"y_bank{a}") for a, b in HALVES}
+        y_bank = {a: psum.tile([P, b - a], F32, name=f"y_bank{a}") for a, b in Y_PIECES}
         gate_bank = {a: psum.tile([P, b - a], F32, name=f"gate_bank{a}") for a, b in HALVES}
-        for a, b in HALVES:
+        for a, b in Y_PIECES:
             product(y_bank[a], "w1", 0, a, b)
-        for a, b in HALVES:
+        for a, b in Y_PIECES:
             product(y_bank[a], "w1", 1, a, b)
             nc.scalar.activation(y[:, a:b], y_bank[a][:], ACT.Tanh)
+        split = S - SCALAR_ENTRIES
+        picked = tile([P, SCALAR_ENTRIES], F32, "picked")
+        nc.scalar.activation(picked[:], res_table[:].indirect(entries(split, S)), ACT.Copy)
         for a, b in HALVES:
             product(gate_bank[a], "w2", 0, a, b)
         for a, b in HALVES:
@@ -136,8 +141,9 @@ def tile_picked_highway_tanh_p_kernel(tc, x_words, x_scales, res, w1, w2, offs, 
         diff = tile([P, S], F32, "diff")
         gated = tile([P, S], F32, "gated")
         result = tile([P, S], F32, "result")
-        for a, b in HALVES:
+        for a, b in ((0, S // 2), (S // 2, split)):
             nc.vector.tensor_tensor(diff[:, a:b], res_table[:].indirect(entries(a, b)), y[:, a:b], ALU.subtract)
+        nc.vector.tensor_tensor(diff[:, split:], picked[:], y[:, split:], ALU.subtract)
         for a, b in HALVES:
             nc.vector.scalar_tensor_tensor(gated[:, a:b], half_tanh[:, a:b], -1.0, diff[:, a:b], ALU.add, ALU.mult)
         for a, b in HALVES:

@@ -126,6 +126,16 @@ def tile_picked_highway_tanh_p_kernel(tc, x_words, x_scales, res, w1, w2, offs, 
         gate_bank = {a: psum.tile([P, b - a], F32, name=f"gate_bank{a}") for a, b in HALVES}
         for a, b in Y_PIECES:
             product(y_bank[a], "w1", 0, a, b)
+        unused = psum.tile([P, N], F32, name="unused")
+        nc.tensor.matmul_mx(
+            out=unused[:],
+            lhsT=w_codes["w1", 0][:].bitcast(FP8X4),
+            lhsT_scale=w_scale["w1", 0][:],
+            rhs=w_codes["w1", 0][:].bitcast(FP8X4),
+            rhs_scale=w_scale["w1", 0][:],
+            start=True,
+            stop=True,
+        )
         for a, b in Y_PIECES:
             product(y_bank[a], "w1", 1, a, b)
             nc.scalar.activation(y[:, a:b], y_bank[a][:], ACT.Tanh)

@@ -36,7 +36,7 @@ def tile_picked_highway_tanh_p_kernel(tc, x_words, x_scales, res, w1, w2, offs, 
         psum = ctx.enter_context(tc.psum_pool(name="psum", bufs=1))
 
         def tile(shape, dtype, name, tag=None):
-            return keep.tile(shape, dtype, name=name, tag=tag or name, align_bytes=64)
+            return keep.tile(shape, dtype, name=name, tag=tag or name, align_bytes=256)
 
         offsets = keep.tile([P, S // LIST_GROUP], U16, name="offsets")
 

from contextlib import ExitStack

import concourse.mybir as mybir

K, T, S, N = 1024, 1024, 512, 128
FLOPS = 2 * 2 * K * N * S

F32 = mybir.dt.float32
BF16 = mybir.dt.bfloat16
I32 = mybir.dt.int32
U32 = mybir.dt.uint32
U16 = mybir.dt.uint16
U8 = mybir.dt.uint8
FP8X4 = mybir.dt.float8_e4m3fn_x4
ACT = mybir.ActivationFunctionType
ALU = mybir.AluOpType

P = 128
PACK = 4
K_PASS = P * PACK
PASSES = K // K_PASS
QUADRANT = 32
SCALE_ROWS = 4
LIST_GROUP = 16
LINE = 4
HALVES = ((0, S // 2), (S // 2, S))
Y_PIECES = ((0, S // 2), (S // 2, 3 * S // 4), (3 * S // 4, S))
SCALAR_ENTRIES = 192


def tile_picked_highway_tanh_p_kernel(tc, x_words, x_scales, res, w1, w2, offs, out):
    nc = tc.nc
    weights = {"w1": w1, "w2": w2}
    with ExitStack() as ctx:
        keep = ctx.enter_context(tc.tile_pool(name="keep", bufs=1))
        psum = ctx.enter_context(tc.psum_pool(name="psum", bufs=1))

        def tile(shape, dtype, name, tag=None):
            return keep.tile(shape, dtype, name=name, tag=tag or name, align_bytes=256)

        offsets = keep.tile([P, S // LIST_GROUP], U16, name="offsets")

        def entries(a, b):
            return offsets[:, a // LIST_GROUP : b // LIST_GROUP]

        scale_table = tile([P, T], U8, "scale_table")
        word_table = [tile([P, T], I32, f"word_table{z}") for z in range(PASSES)]
        raw = {(name, z): tile([P, PACK, N], F32, f"raw_{name}_{z}") for name in weights for z in range(PASSES)}
        res_table = tile([P, T], F32, "res_table")

        def load_words(z):
            nc.sync.dma_start(word_table[z][:], x_words[z].rearrange("p n t -> p (n t)").bitcast(I32))

        def load_scales(q):
            nc.sync.dma_start(
                scale_table[QUADRANT * q : QUADRANT * q + SCALE_ROWS * PASSES, :].bitcast(I32),
                x_scales[:, SCALE_ROWS * q : SCALE_ROWS * (q + 1), :].bitcast(I32),
            )

        def load_weight(name, z):
            rows = weights[name][z * K_PASS : (z + 1) * K_PASS, :]
            nc.sync.dma_start(raw[name, z][:], rows.rearrange("(p j) m -> p j m", j=PACK))

        x_scale = tile([P, S], U8, "x_scale")
        grouped = {}
        w_codes = {}
        w_scale = {}
        for name in weights:
            for z in range(PASSES):
                grouped[name, z] = tile([P, N, PACK], BF16, f"grouped_{name}_{z}")
                w_codes[name, z] = tile([P, N], U32, f"codes_{name}_{z}")
                w_scale[name, z] = tile([P, N], U8, f"scale_{name}_{z}")

        def cast_and_quantize(name, z):
            nc.scalar.activation(
                grouped[name, z][:].rearrange("p (c i) j -> p c j i", i=LINE),
                raw[name, z][:].rearrange("p j (c i) -> p c j i", i=LINE),
                ACT.Copy,
            )
            nc.vector.quantize_mx(
                out=w_codes[name, z][:].bitcast(FP8X4),
                scales=w_scale[name, z][:],
                in_=grouped[name, z][:].rearrange("p m j -> p (m j)"),
            )

        x_codes = {}

        def product(bank, name, z, a, b):
            nc.tensor.matmul_mx(
                out=bank[:],
                lhsT=w_codes[name, z][:].bitcast(FP8X4),
                lhsT_scale=w_scale[name, z][:],
                rhs=x_codes[z][:, a:b].bitcast(FP8X4),
                rhs_scale=x_scale[SCALE_ROWS * z : P, a:b],
                start=(z == 0),
                stop=(z == PASSES - 1),
            )

        nc.vector.memset(scale_table[:].bitcast(I32), 0)

        load_words(0)
        nc.sync.dma_start(offsets[:], offs)
        for q in (0, 2, 1, 3):
            load_scales(q)
        load_weight("w1", 0)
        load_weight("w1", 1)
        load_words(1)
        load_weight("w2", 0)
        load_weight("w2", 1)
        nc.sync.dma_start(res_table[:], res)

        x_codes[0] = tile([P, S], U32, "x_first")
        nc.vector.tensor_copy(x_codes[0][:], word_table[0][:].bitcast(U32).indirect(offsets[:]))
        nc.vector.tensor_copy(x_scale[:], scale_table[:].indirect(offsets[:]))
        for z in range(PASSES):
            cast_and_quantize("w1", z)
        x_codes[1] = tile([P, S], U32, "x_second", tag="raw_w1_1")
        for a, b in Y_PIECES:
            nc.vector.tensor_copy(x_codes[1][:, a:b], word_table[1][:].bitcast(U32).indirect(entries(a, b)))
        for z in range(PASSES):
            cast_and_quantize("w2", z)

        y = tile([P, S], F32, "y", tag="raw_w2_0")
        half_tanh = tile([P, S], F32, "half_tanh")
        y_bank = {a: psum.tile([P, b - a], F32, name=f"y_bank{a}") for a, b in Y_PIECES}
        gate_bank = {a: psum.tile([P, b - a], F32, name=f"gate_bank{a}") for a, b in HALVES}
        for a, b in Y_PIECES:
            product(y_bank[a], "w1", 0, a, b)
        unused = psum.tile([P, N], F32, name="unused")
        nc.tensor.matmul_mx(
            out=unused[:],
            lhsT=w_codes["w1", 0][:].bitcast(FP8X4),
            lhsT_scale=w_scale["w1", 0][:],
            rhs=w_codes["w1", 0][:].bitcast(FP8X4),
            rhs_scale=w_scale["w1", 0][:],
            start=True,
            stop=True,
        )
        for a, b in Y_PIECES:
            product(y_bank[a], "w1", 1, a, b)
            nc.scalar.activation(y[:, a:b], y_bank[a][:], ACT.Tanh)
        split = S - SCALAR_ENTRIES
        picked = tile([P, SCALAR_ENTRIES], F32, "picked")
        nc.scalar.activation(picked[:], res_table[:].indirect(entries(split, S)), ACT.Copy)
        for a, b in HALVES:
            product(gate_bank[a], "w2", 0, a, b)
        for a, b in HALVES:
            product(gate_bank[a], "w2", 1, a, b)
            nc.scalar.activation(half_tanh[:, a:b], gate_bank[a][:], ACT.Tanh, scale=0.5)

        diff = tile([P, S], F32, "diff")
        gated = tile([P, S], F32, "gated")
        result = tile([P, S], F32, "result")
        for a, b in ((0, S // 2), (S // 2, split)):
            nc.vector.tensor_tensor(diff[:, a:b], res_table[:].indirect(entries(a, b)), y[:, a:b], ALU.subtract)
        nc.vector.tensor_tensor(diff[:, split:], picked[:], y[:, split:], ALU.subtract)
        for a, b in HALVES:
            nc.vector.scalar_tensor_tensor(gated[:, a:b], half_tanh[:, a:b], -1.0, diff[:, a:b], ALU.add, ALU.mult)
        for a, b in HALVES:
            nc.vector.scalar_tensor_tensor(result[:, a:b], gated[:, a:b], -0.5, y[:, a:b], ALU.mult, ALU.add)
            nc.sync.dma_start(out[:, a:b], result[:, a:b])
